import numpy as np
import ml_dtypes


def mxq(x, axis, fmt="e4m3"):
    dtype, down = {"e4m3": (ml_dtypes.float8_e4m3fn, 7), "e5m2": (ml_dtypes.float8_e5m2, 14)}[fmt]
    v = np.moveaxis(np.asarray(x, np.float32).astype(ml_dtypes.bfloat16).astype(np.float64), axis, -1)
    blocks = v.reshape(v.shape[:-1] + (-1, 32))
    amax = np.abs(blocks).max(-1, keepdims=True)
    byte = np.maximum(np.where(amax > 0, np.frexp(amax)[1] - 1 + 127, 0) - down, 1)
    scale = np.exp2(byte - 127.0)
    codes = (blocks / scale).astype(np.float32).astype(dtype).astype(np.float64)
    return np.moveaxis((codes * scale).reshape(v.shape), -1, axis)


WIDE = False


def mx_kscale(k):
    if not WIDE:
        return np.ones(k)
    levels = np.array([10, -10, 5, -5, 0])
    if k % 512:
        return np.exp2(np.random.permutation(np.resize(levels, k // 32))).repeat(32)
    a = np.empty((k // 512, 16))
    for p in range(k // 512):
        a[p, :8] = np.random.permutation(np.resize(levels, 8))
        for g in range(8):
            far = levels[np.abs(levels - a[p, g]) >= 10]
            a[p, g + 8] = far[np.random.randint(len(far))]
    return np.exp2(a.ravel()).repeat(32)


def f64(x):
    return np.asarray(x).astype(np.float64)


def striped(idx):
    return np.tile(idx.reshape(-1, 16).T, (8, 1)).astype(np.uint16)


def unstriped(offs):
    return offs[:16].T.reshape(-1).astype(np.int64)


E2M1 = np.array([0.0, 0.5, 1.0, 1.5, 2.0, 3.0, 4.0, 6.0, -0.0, -0.5, -1.0, -1.5, -2.0, -3.0, -4.0, -6.0])


def pack_weight(w, fmt):
    k, n = w.shape
    w = f64(np.asarray(w, np.float32).astype(ml_dtypes.bfloat16)).reshape(k // 32, 32, n)
    amax = np.abs(w).max(1)
    if fmt == "e4m3":
        byte = np.frexp(amax)[1] - 1 + 127 - 7
    else:
        mant, ex = np.frexp(amax / 6.0)
        byte = np.where(mant > 0.5, ex, ex - 1) + 127
    byte = np.clip(np.where(amax > 0, byte, 1), 1, 254)
    scaled = (w * np.exp2(127.0 - byte)[:, None, :]).reshape(k, n).astype(np.float32)
    by_word = np.ascontiguousarray(scaled.reshape(k // 512, 128, 4, n).transpose(0, 1, 3, 2))
    if fmt == "e4m3":
        words = by_word.astype(ml_dtypes.float8_e4m3fn).view(np.uint8)
    else:
        c = by_word.astype(ml_dtypes.float4_e2m1fn).view(np.uint8) & 0xF
        words = (c[..., 0::2] | (c[..., 1::2] << 4)).reshape(k // 512, 128, 2 * n)
    return np.ascontiguousarray(words), np.ascontiguousarray(byte.astype(np.uint8).reshape(k // 512, 16, n))


def unpack_weight(words, scales, fmt):
    g, _, n = scales.shape
    words = np.ascontiguousarray(words).reshape(g, 128, n, -1)
    if fmt == "e4m3":
        vals = words.view(ml_dtypes.float8_e4m3fn).astype(np.float64)
    else:
        nib = np.empty((g, 128, n, 4), np.uint8)
        nib[..., 0::2] = words & 0xF
        nib[..., 1::2] = words >> 4
        vals = E2M1[nib]
    vals = vals * np.repeat(np.exp2(scales.astype(np.float64) - 127.0), 8, axis=1)[..., None]
    return vals.transpose(0, 1, 3, 2).reshape(g * 512, n)


def gelu(v):
    return 0.5 * v * (1.0 + np.tanh(np.sqrt(2.0 / np.pi) * (v + 0.044715 * v**3)))


K, T, H, N, S, T2 = 1024, 4096, 512, 768, 1024, 2048

def setup_inputs():
    n = np.random.standard_normal
    s = mx_kscale(K)[:, None]
    u = mx_kscale(H)[:, None]
    tab_words, tab_scales = pack_weight(n((K, T)) * s, "e4m3")
    wb_words, wb_scales = pack_weight(n((K, H)) / np.sqrt(K) / s * u.T, "e2m1")
    wd_words, wd_scales = pack_weight(1.2 * n((K, N)) / np.sqrt(K) / s, "e4m3")
    return {
        "tab_words": tab_words, "tab_scales": tab_scales,
        "wa": (n((K, H)) / np.sqrt(K) / s * u.T).astype(np.float32),
        "wb_words": wb_words, "wb_scales": wb_scales,
        "wc": (1.3 * n((H, N)) / np.sqrt(H) / u).astype(np.float32),
        "bc": (0.5 * n(N)).astype(np.float32),
        "wd_words": wd_words, "wd_scales": wd_scales,
        "wgo": np.exp(0.3 * n((128, S))).astype(np.float32),
        "offs": striped(np.random.permutation(T)[:S]),
        "offs2": striped(np.random.permutation(T)[:S]),
        "offs3": striped(np.random.permutation(T2)[:S]),
    }

def reference(tab_words, tab_scales, wa, wb_words, wb_scales, wc, bc, wd_words, wd_scales, wgo, offs, offs2, offs3):
    TW = unpack_weight(tab_words, tab_scales, "e4m3")
    v = TW[:, unstriped(offs)]
    v2 = TW[:, unstriped(offs2)]
    wb = unpack_weight(wb_words, wb_scales, "e2m1")
    wd = unpack_weight(wd_words, wd_scales, "e4m3")
    feed = mxq(f64(wa), 0, "e4m3").T @ v
    dep = wb.T @ v2
    h = np.minimum(feed, dep)
    hold = np.tanh((mxq(f64(wc), 0, "e4m3").T @ mxq(h, 0, "e4m3")) + f64(bc)[:, None])
    load = wd.T @ v
    y = hold / (1.0 + np.abs(load))
    out = np.zeros((N, T2))
    out[:, unstriped(offs3)] = np.tile(f64(wgo), (N // 128, 1)) * y
    return out

@@ -1,0 +1,287 @@
+from contextlib import ExitStack
+
+import concourse.mybir as mybir
+
+K, T, H, N, S, T2 = 1024, 4096, 512, 768, 1024, 2048
+FLOPS = 2 * S * (K * H + K * H + K * N + H * N)
+
+F32 = mybir.dt.float32
+BF16 = mybir.dt.bfloat16
+I32 = mybir.dt.int32
+U32 = mybir.dt.uint32
+U16 = mybir.dt.uint16
+U8 = mybir.dt.uint8
+FP8X4 = mybir.dt.float8_e4m3fn_x4
+FP4X4 = mybir.dt.float4_e2m1fn_x4
+ACT = mybir.ActivationFunctionType
+ALU = mybir.AluOpType
+
+P = 128
+PASSES = K // 512
+HALF = 512
+CHUNK = 128
+ROW_TILES = N // P
+GROUP = 2
+FIRST = GROUP * P
+PAGES = 2
+
+
+def tile_list_connection_hold_scores_kernel(
+    tc, tab_words, tab_scales, wa, wb_words, wb_scales, wc, bc, wd_words, wd_scales, wgo, offs, offs2, offs3, out
+):
+    nc = tc.nc
+    with ExitStack() as ctx:
+        keep = ctx.enter_context(tc.tile_pool(name="keep", bufs=1))
+        psum = ctx.enter_context(tc.psum_pool(name="psum", bufs=1))
+
+        def sb(name, shape, dtype):
+            return keep.tile(shape, dtype, name=name, align_bytes=64)
+
+        list1 = keep.tile([P, S // 16], U16, name="list1")
+        list2 = keep.tile([P, S // 16], U16, name="list2")
+        list3 = keep.tile([P, S // 16], U16, name="list3")
+        tabw = [sb("tabw%d" % a, [P, T], I32) for a in range(PASSES)]
+        tabs = sb("tabs", [P, T // 4], I32)
+        v1w = [sb("v1w%d" % a, [P, S], U32) for a in range(PASSES)]
+        v2w = [sb("v2w%d" % a, [P, S], U32) for a in range(PASSES)]
+        v1g = sb("v1g", [P, S], U8)
+        v2g = sb("v2g", [P, S], U8)
+        v1s = sb("v1s", [P, PASSES * S], U8)
+        v2s = sb("v2s", [P, PASSES * S], U8)
+        wa_raw = [sb("wa_raw%d" % a, [P, 4, H], F32) for a in range(PASSES)]
+        wa_bf = [sb("wa_bf%d" % a, [P, 4 * H], BF16) for a in range(PASSES)]
+        wa_q = [sb("wa_q%d" % a, [P, H], U32) for a in range(PASSES)]
+        wa_s = [sb("wa_s%d" % a, [P, H], U8) for a in range(PASSES)]
+        wb_raw = sb("wb_raw", [P, PASSES, H // 2], I32)
+        wbs_raw = sb("wbs_raw", [P, PASSES, H // 4], I32)
+        wb_q = sb("wb_q", [P, PASSES * 2 * H], U8)
+        wb_s = sb("wb_s", [P, PASSES * H], U8)
+        widths = [FIRST, N - FIRST]
+        starts = [0, FIRST]
+        wc_raw = [sb("wc_raw%d" % u, [P, 4, widths[u]], F32) for u in range(2)]
+        wc_q = [sb("wc_q%d" % u, [P, widths[u]], U32) for u in range(2)]
+        wc_s = [sb("wc_s%d" % u, [P, widths[u]], U8) for u in range(2)]
+        wd_q = [sb("wd_q%d" % u, [P, PASSES, widths[u]], I32) for u in range(2)]
+        wd_s = sb("wd_s", [P, PASSES * N], U8)
+        bias = sb("bias", [P, ROW_TILES], F32)
+        gain = sb("gain", [P, S], F32)
+        dep_sb = [sb("dep_sb%d" % c, [P, 4 * CHUNK], F32) for c in range(S // CHUNK)]
+        h_bf = [sb("h_bf%d" % b, [P, 4 * HALF], BF16) for b in range(2)]
+        wc_bf = [sb("wc_bf0", [P, 4 * FIRST], BF16), h_bf[1]]
+        h_q = [sb("h_q%d" % b, [P, HALF], U32) for b in range(2)]
+        h_s = [sb("h_s%d" % b, [P, HALF], U8) for b in range(2)]
+        damp = [sb("damp%d" % i, [P, S], F32) for i in range(2 * GROUP)]
+        hold = [sb("hold%d" % i, [P, S], F32) for i in range(2 * GROUP)]
+        ys = [sb("y%d" % i, [P, S], F32) for i in range(2)]
+        pages = [sb("page%d" % i, [P, T2], F32) for i in range(PAGES)]
+        dep_ps = [psum.tile([P, 4, CHUNK], F32, name="dep_ps%d" % i) for i in range(2)]
+        feed_ps = [psum.tile([P, 4, CHUNK], F32, name="feed_ps%d" % i) for i in range(2)]
+        row_ps = [psum.tile([P, HALF], F32, name="row_ps%d" % i) for i in range(2 * GROUP)]
+
+        nc.gpsimd.memset(tabs[32:64, :], 0)
+        nc.gpsimd.memset(tabs[64:P, :], 0)
+        nc.vector.memset(wbs_raw[:], 0)
+        for page in pages:
+            nc.vector.memset(page[:], 0.0)
+
+        nc.sync.dma_start(tabs[0:32, :], tab_scales.rearrange("a q c -> q a c").bitcast(I32))
+        nc.sync.dma_start(list1[:], offs)
+        nc.sync.dma_start(list2[:], offs2)
+        nc.sync.dma_start(tabw[0][:], tab_words[0].rearrange("p t i -> p (t i)").bitcast(I32))
+        for q in range(4):
+            nc.sync.dma_start(
+                wd_s[32 * q : 32 * q + 4, :].rearrange("r (a c) -> r a c", a=PASSES).bitcast(I32),
+                wd_scales[:, 4 * q : 4 * q + 4, :].rearrange("a r c -> r a c").bitcast(I32),
+            )
+        nc.sync.dma_start(tabw[1][:], tab_words[1].rearrange("p t i -> p (t i)").bitcast(I32))
+        for q in range(4):
+            nc.sync.dma_start(
+                wbs_raw[32 * q : 32 * q + 4, :, :],
+                wb_scales[:, 4 * q : 4 * q + 4, :].rearrange("a r c -> r a c").bitcast(I32),
+            )
+        wd_view = wd_words.rearrange("a p c i -> p a (c i)").bitcast(I32)
+        nc.sync.dma_start(wd_q[0][:], wd_view[:, :, 0:FIRST])
+        nc.sync.dma_start(wb_raw[:], wb_words.rearrange("a p c -> p a c").bitcast(I32))
+        for a in range(PASSES):
+            nc.sync.dma_start(wa_raw[a][:], wa[512 * a : 512 * (a + 1), :].rearrange("(p i) c -> p i c", i=4))
+        wc_view = wc.rearrange("(g t e) n -> t g e n", t=4, e=8)
+        for t in range(4):
+            nc.sync.dma_start(wc_raw[0][:, t, :], wc_view[t][:, :, 0:FIRST])
+        nc.sync.dma_start(gain[:], wgo)
+        nc.sync.dma_start(list3[:], offs3)
+        with nc.allow_non_contiguous_dma(reason="one bias value a partition and row tile"):
+            nc.sync.dma_start(bias[:], bc.rearrange("(i p) -> p i", p=P))
+        nc.sync.dma_start(wd_q[1][:], wd_view[:, :, FIRST:N])
+        for t in range(4):
+            nc.sync.dma_start(wc_raw[1][:, t, :], wc_view[t][:, :, FIRST:N])
+
+        def cols16(b):
+            return slice(b * HALF // 16, (b + 1) * HALF // 16)
+
+        def cols(b):
+            return slice(b * HALF, (b + 1) * HALF)
+
+        for picked, plane, lst in ((v1g, v1s, list1), (v2g, v2s, list2)):
+            nc.vector.tensor_copy(picked[:], tabs[:].bitcast(U8).indirect(lst[:]))
+            for q in range(4):
+                nc.gpsimd.dma_start(
+                    plane[32 * q : 32 * q + 4, :].bitcast(I32).rearrange("r (a w) -> r a w", a=PASSES),
+                    picked[8 * q : 8 * q + 8, :].bitcast(I32),
+                )
+        nc.vector.tensor_copy(v1w[0][:], tabw[0][:].bitcast(U32).indirect(list1[:]))
+        nc.vector.tensor_copy(v2w[0][:], tabw[0][:].bitcast(U32).indirect(list2[:]))
+        for b in range(2):
+            nc.vector.tensor_copy(v1w[1][:, cols(b)], tabw[1][:].bitcast(U32).indirect(list1[:, cols16(b)]))
+
+        nc.vector.tensor_copy(
+            wb_q[:].bitcast(I32).rearrange("p (a t g w) -> p a t g w", a=PASSES, t=4, w=4),
+            wb_raw[:].rearrange("p a (g t w) -> p a t g w", t=4, w=4),
+        )
+        nc.vector.tensor_copy(
+            wb_s[:].bitcast(I32).rearrange("p (a t g w) -> p a t g w", a=PASSES, t=4, w=2),
+            wbs_raw[:].rearrange("p a (g t w) -> p a t g w", t=4, w=2),
+        )
+        for b in range(2):
+            nc.vector.tensor_copy(v2w[1][:, cols(b)], tabw[1][:].bitcast(U32).indirect(list2[:, cols16(b)]))
+
+        def part(i):
+            u = 0 if i < GROUP else 1
+            return u, slice(i * P - starts[u], (i + 1) * P - starts[u])
+
+        def load_logs(g):
+            for b in range(2):
+                for r in range(GROUP):
+                    i = g * GROUP + r
+                    u, ncols = part(i)
+                    bank = row_ps[2 * r + b]
+                    for a in range(PASSES):
+                        nc.tensor.matmul_mx(
+                            out=bank[:],
+                            lhsT=wd_q[u][:, a, ncols].bitcast(FP8X4),
+                            lhsT_scale=wd_s[:, a * N + i * P : a * N + (i + 1) * P],
+                            rhs=v1w[a][:, cols(b)].bitcast(FP8X4),
+                            rhs_scale=v1s[:, a * S + b * HALF : a * S + (b + 1) * HALF],
+                            start=(a == 0),
+                            stop=(a == PASSES - 1),
+                        )
+                    nc.scalar.activation(damp[i % len(damp)][:, cols(b)], bank[:], ACT.Abs)
+            for r in range(GROUP):
+                d = damp[(g * GROUP + r) % len(damp)]
+                nc.scalar.activation(d[:], d[:], ACT.Ln, bias=1.0)
+
+        def round_wc(u, engine_copy):
+            engine_copy(
+                wc_bf[u][:].rearrange("p (n t) -> p n t", t=4),
+                wc_raw[u][:].rearrange("p t n -> p n t"),
+            )
+
+        def quantise_wc(u):
+            nc.vector.quantize_mx(out=wc_q[u][:].bitcast(FP8X4), scales=wc_s[u][:], in_=wc_bf[u][:])
+
+        load_logs(0)
+
+        for a in range(PASSES):
+            nc.vector.tensor_copy(
+                wa_bf[a][:].rearrange("p (t g e i) -> p t g e i", t=4, e=8, i=4),
+                wa_raw[a][:].rearrange("p i (g t e) -> p t g e i", t=4, e=8),
+            )
+        for a in range(PASSES):
+            nc.vector.quantize_mx(out=wa_q[a][:].bitcast(FP8X4), scales=wa_s[a][:], in_=wa_bf[a][:])
+
+        dep_banks = dep_ps + [r[:].rearrange("p (t j) -> p t j", t=4) for r in row_ps] + dep_ps
+
+        def departure(c):
+            bank = dep_banks[c]
+            for t in range(4):
+                for a in range(PASSES):
+                    c0 = a * H + t * P
+                    nc.tensor.matmul_mx(
+                        out=bank[:, t, :],
+                        lhsT=wb_q[:, 2 * c0 : 2 * (c0 + P)].bitcast(FP4X4),
+                        lhsT_scale=wb_s[:, c0 : c0 + P],
+                        rhs=v2w[a][:, c * CHUNK : (c + 1) * CHUNK].bitcast(FP8X4),
+                        rhs_scale=v2s[:, a * S + c * CHUNK : a * S + (c + 1) * CHUNK],
+                        start=(a == 0),
+                        stop=(a == PASSES - 1),
+                    )
+            nc.scalar.copy(dep_sb[c][:].rearrange("p (j t) -> p j t", t=4), bank[:].rearrange("p t j -> p j t"))
+
+        AHEAD = 6
+        for c in range(AHEAD):
+            departure(c)
+        for c in range(S // CHUNK):
+            bank = feed_ps[c % 2]
+            for t in range(4):
+                for a in range(PASSES):
+                    nc.tensor.matmul_mx(
+                        out=bank[:, t, :],
+                        lhsT=wa_q[a][:, t * P : (t + 1) * P].bitcast(FP8X4),
+                        lhsT_scale=wa_s[a][:, t * P : (t + 1) * P],
+                        rhs=v1w[a][:, c * CHUNK : (c + 1) * CHUNK].bitcast(FP8X4),
+                        rhs_scale=v1s[:, a * S + c * CHUNK : a * S + (c + 1) * CHUNK],
+                        start=(a == 0),
+                        stop=(a == PASSES - 1),
+                    )
+            if c + AHEAD < S // CHUNK:
+                departure(c + AHEAD)
+            b, w = divmod(c, HALF // CHUNK)
+            nc.vector.tensor_tensor(
+                h_bf[b][:, 4 * CHUNK * w : 4 * CHUNK * (w + 1)].rearrange("p (j t) -> p j t", t=4),
+                bank[:].rearrange("p t j -> p j t"),
+                dep_sb[c][:].rearrange("p (j t) -> p j t", t=4),
+                ALU.min,
+            )
+            if c == 0:
+                round_wc(0, nc.vector.tensor_copy)
+            if c == 1:
+                quantise_wc(0)
+            if c == HALF // CHUNK:
+                nc.vector.quantize_mx(out=h_q[0][:].bitcast(FP8X4), scales=h_s[0][:], in_=h_bf[0][:])
+        nc.vector.quantize_mx(out=h_q[1][:].bitcast(FP8X4), scales=h_s[1][:], in_=h_bf[1][:])
+
+
+        def scores(g):
+            for r in range(GROUP):
+                i = g * GROUP + r
+                u, ncols = part(i)
+                d = damp[i % len(damp)]
+                for b in range(2):
+                    nc.scalar.activation(d[:, cols(b)], d[:, cols(b)], ACT.Exp, scale=-1.0)
+                    bank = row_ps[2 * r + b]
+                    nc.tensor.matmul_mx(
+                        out=bank[:],
+                        lhsT=wc_q[u][:, ncols].bitcast(FP8X4),
+                        lhsT_scale=wc_s[u][:, ncols],
+                        rhs=h_q[b][:].bitcast(FP8X4),
+                        rhs_scale=h_s[b][:],
+                        start=True,
+                        stop=True,
+                    )
+                    nc.scalar.activation(
+                        hold[i % len(hold)][:, cols(b)], bank[:], ACT.Tanh, bias=bias[:, i : i + 1]
+                    )
+
+        def place(g):
+            for r in range(GROUP):
+                i = g * GROUP + r
+                y = ys[i % len(ys)]
+                page = pages[i % PAGES]
+                for b in range(2):
+                    nc.vector.tensor_tensor(
+                        y[:, cols(b)], hold[i % len(hold)][:, cols(b)], damp[i % len(damp)][:, cols(b)], ALU.mult
+                    )
+                for b in range(2):
+                    nc.vector.tensor_tensor(
+                        page[:].indirect(list3[:, cols16(b)]), y[:, cols(b)], gain[:, cols(b)], ALU.mult
+                    )
+                nc.sync.dma_start(out[i * P : (i + 1) * P, :], page[:])
+                if i == 0:
+                    quantise_wc(1)
+
+        for g in range(ROW_TILES // GROUP):
+            scores(g)
+            if g == 0:
+                round_wc(1, nc.scalar.copy)
+            if g + 1 < ROW_TILES // GROUP:
+                load_logs(g + 1)
+            place(g)

@@ -67,7 +67,7 @@ def tile_list_connection_hold_scores_kernel(
         gain = sb("gain", [P, S], F32)
         dep_sb = [sb("dep_sb%d" % c, [P, 4 * CHUNK], F32) for c in range(S // CHUNK)]
         h_bf = [sb("h_bf%d" % b, [P, 4 * HALF], BF16) for b in range(2)]
-        wc_bf = [sb("wc_bf0", [P, 4 * FIRST], BF16), h_bf[1]]
+        wc_bf = [sb("wc_bf%d" % u, [P, 4 * widths[u]], BF16) for u in range(2)]
         h_q = [sb("h_q%d" % b, [P, HALF], U32) for b in range(2)]
         h_s = [sb("h_s%d" % b, [P, HALF], U8) for b in range(2)]
         damp = [sb("damp%d" % i, [P, S], F32) for i in range(2 * GROUP)]
@@ -78,9 +78,9 @@ def tile_list_connection_hold_scores_kernel(
         feed_ps = [psum.tile([P, 4, CHUNK], F32, name="feed_ps%d" % i) for i in range(2)]
         row_ps = [psum.tile([P, HALF], F32, name="row_ps%d" % i) for i in range(2 * GROUP)]
 
-        nc.gpsimd.memset(tabs[32:64, :], 0)
-        nc.gpsimd.memset(tabs[64:P, :], 0)
-        nc.vector.memset(wbs_raw[:], 0)
+        nc.vector.memset(tabs[32:64, :], 0)
+        nc.vector.memset(tabs[64:P, :], 0)
+        nc.gpsimd.memset(wbs_raw[:], 0)
         for page in pages:
             nc.vector.memset(page[:], 0.0)
 
@@ -94,14 +94,14 @@ def tile_list_connection_hold_scores_kernel(
                 wd_scales[:, 4 * q : 4 * q + 4, :].rearrange("a r c -> r a c").bitcast(I32),
             )
         nc.sync.dma_start(tabw[1][:], tab_words[1].rearrange("p t i -> p (t i)").bitcast(I32))
-        for q in range(4):
-            nc.sync.dma_start(
-                wbs_raw[32 * q : 32 * q + 4, :, :],
-                wb_scales[:, 4 * q : 4 * q + 4, :].rearrange("a r c -> r a c").bitcast(I32),
-            )
         wd_view = wd_words.rearrange("a p c i -> p a (c i)").bitcast(I32)
         nc.sync.dma_start(wd_q[0][:], wd_view[:, :, 0:FIRST])
         nc.sync.dma_start(wb_raw[:], wb_words.rearrange("a p c -> p a c").bitcast(I32))
+        for q in range(4):
+            nc.gpsimd.dma_start(
+                wbs_raw[32 * q : 32 * q + 4, :, :],
+                wb_scales[:, 4 * q : 4 * q + 4, :].rearrange("a r c -> r a c").bitcast(I32),
+            )
         for a in range(PASSES):
             nc.sync.dma_start(wa_raw[a][:], wa[512 * a : 512 * (a + 1), :].rearrange("(p i) c -> p i c", i=4))
         wc_view = wc.rearrange("(g t e) n -> t g e n", t=4, e=8)
@@ -121,10 +121,10 @@ def tile_list_connection_hold_scores_kernel(
         def cols(b):
             return slice(b * HALF, (b + 1) * HALF)
 
-        for picked, plane, lst in ((v1g, v1s, list1), (v2g, v2s, list2)):
+        for picked, plane, lst, queue in ((v1g, v1s, list1, nc.scalar), (v2g, v2s, list2, nc.gpsimd)):
             nc.vector.tensor_copy(picked[:], tabs[:].bitcast(U8).indirect(lst[:]))
             for q in range(4):
-                nc.gpsimd.dma_start(
+                queue.dma_start(
                     plane[32 * q : 32 * q + 4, :].bitcast(I32).rearrange("r (a w) -> r a w", a=PASSES),
                     picked[8 * q : 8 * q + 8, :].bitcast(I32),
                 )
@@ -240,6 +240,16 @@ def tile_list_connection_hold_scores_kernel(
         nc.vector.quantize_mx(out=h_q[1][:].bitcast(FP8X4), scales=h_s[1][:], in_=h_bf[1][:])
 
 
+        for n0 in range(0, widths[1], FIRST):
+            nc.gpsimd.tensor_scalar(
+                wc_bf[1][:, 4 * n0 : 4 * (n0 + FIRST)].rearrange("p (n t) -> p n t", t=4),
+                wc_raw[1][:, :, n0 : n0 + FIRST].rearrange("p t n -> p n t"),
+                1.0,
+                0.0,
+                ALU.mult,
+                ALU.add,
+            )
+
         def scores(g):
             for r in range(GROUP):
                 i = g * GROUP + r
@@ -267,21 +277,18 @@ def tile_list_connection_hold_scores_kernel(
                 y = ys[i % len(ys)]
                 page = pages[i % PAGES]
                 for b in range(2):
-                    nc.vector.tensor_tensor(
+                    engine = nc.vector if (i, b) == (0, 0) else nc.gpsimd
+                    engine.tensor_tensor(
                         y[:, cols(b)], hold[i % len(hold)][:, cols(b)], damp[i % len(damp)][:, cols(b)], ALU.mult
                     )
-                for b in range(2):
-                    nc.vector.tensor_tensor(
-                        page[:].indirect(list3[:, cols16(b)]), y[:, cols(b)], gain[:, cols(b)], ALU.mult
-                    )
+                    engine.tensor_tensor(y[:, cols(b)], y[:, cols(b)], gain[:, cols(b)], ALU.mult)
+                    nc.vector.tensor_copy(page[:].indirect(list3[:, cols16(b)]), y[:, cols(b)])
                 nc.sync.dma_start(out[i * P : (i + 1) * P, :], page[:])
                 if i == 0:
                     quantise_wc(1)
 
         for g in range(ROW_TILES // GROUP):
             scores(g)
-            if g == 0:
-                round_wc(1, nc.scalar.copy)
             if g + 1 < ROW_TILES // GROUP:
                 load_logs(g + 1)
             place(g)

@@ -59,8 +59,8 @@ def tile_list_connection_hold_scores_kernel(
         widths = [FIRST, N - FIRST]
         starts = [0, FIRST]
         wc_raw = [sb("wc_raw%d" % u, [P, 4, widths[u]], F32) for u in range(2)]
-        wc_q = [sb("wc_q%d" % u, [P, widths[u]], U32) for u in range(2)]
-        wc_s = [sb("wc_s%d" % u, [P, widths[u]], U8) for u in range(2)]
+        wc_q = [sb("wc_q0", [P, FIRST], U32), wa_q[0]]
+        wc_s = [sb("wc_s0", [P, FIRST], U8), wa_s[0]]
         wd_q = [sb("wd_q%d" % u, [P, PASSES, widths[u]], I32) for u in range(2)]
         wd_s = sb("wd_s", [P, PASSES * N], U8)
         bias = sb("bias", [P, ROW_TILES], F32)
@@ -70,40 +70,58 @@ def tile_list_connection_hold_scores_kernel(
         wc_bf = [sb("wc_bf%d" % u, [P, 4 * widths[u]], BF16) for u in range(2)]
         h_q = [sb("h_q%d" % b, [P, HALF], U32) for b in range(2)]
         h_s = [sb("h_s%d" % b, [P, HALF], U8) for b in range(2)]
-        damp = [sb("damp%d" % i, [P, S], F32) for i in range(2 * GROUP)]
+        logs = [sb("logs%d" % i, [P, S], F32) for i in range(GROUP)]
         hold = [sb("hold%d" % i, [P, S], F32) for i in range(2 * GROUP)]
-        ys = [sb("y%d" % i, [P, S], F32) for i in range(2)]
+        ys = h_bf[1][:].bitcast(F32)
         pages = [sb("page%d" % i, [P, T2], F32) for i in range(PAGES)]
-        dep_ps = [psum.tile([P, 4, CHUNK], F32, name="dep_ps%d" % i) for i in range(2)]
-        feed_ps = [psum.tile([P, 4, CHUNK], F32, name="feed_ps%d" % i) for i in range(2)]
-        row_ps = [psum.tile([P, HALF], F32, name="row_ps%d" % i) for i in range(2 * GROUP)]
+        banks = [psum.tile([P, HALF], F32, name="bank%d" % i) for i in range(8)]
 
+        nc.vector.memset(wbs_raw[:], 0)
         nc.vector.memset(tabs[32:64, :], 0)
         nc.vector.memset(tabs[64:P, :], 0)
-        nc.gpsimd.memset(wbs_raw[:], 0)
-        for page in pages:
-            nc.vector.memset(page[:], 0.0)
+
+        def cols16(b):
+            return slice(b * HALF // 16, (b + 1) * HALF // 16)
+
+        def cols(b):
+            return slice(b * HALF, (b + 1) * HALF)
+
+        def carry(picked, plane, queue):
+            for q in range(4):
+                queue.dma_start(
+                    plane[32 * q : 32 * q + 4, :].bitcast(I32).rearrange("r (a w) -> r a w", a=PASSES),
+                    picked[8 * q : 8 * q + 8, :].bitcast(I32),
+                )
+
+        def load_wa(a):
+            nc.sync.dma_start(wa_raw[a][:], wa[512 * a : 512 * (a + 1), :].rearrange("(p i) c -> p i c", i=4))
 
         nc.sync.dma_start(tabs[0:32, :], tab_scales.rearrange("a q c -> q a c").bitcast(I32))
-        nc.sync.dma_start(list1[:], offs)
         nc.sync.dma_start(list2[:], offs2)
+        nc.sync.dma_start(list1[:], offs)
+        nc.sync.dma_start(wb_raw[:], wb_words.rearrange("a p c -> p a c").bitcast(I32))
         nc.sync.dma_start(tabw[0][:], tab_words[0].rearrange("p t i -> p (t i)").bitcast(I32))
         for q in range(4):
-            nc.sync.dma_start(
+            nc.gpsimd.dma_start(
                 wd_s[32 * q : 32 * q + 4, :].rearrange("r (a c) -> r a c", a=PASSES).bitcast(I32),
                 wd_scales[:, 4 * q : 4 * q + 4, :].rearrange("a r c -> r a c").bitcast(I32),
             )
-        nc.sync.dma_start(tabw[1][:], tab_words[1].rearrange("p t i -> p (t i)").bitcast(I32))
-        wd_view = wd_words.rearrange("a p c i -> p a (c i)").bitcast(I32)
-        nc.sync.dma_start(wd_q[0][:], wd_view[:, :, 0:FIRST])
-        nc.sync.dma_start(wb_raw[:], wb_words.rearrange("a p c -> p a c").bitcast(I32))
+        for page in pages:
+            nc.gpsimd.memset(page[:], 0.0)
         for q in range(4):
-            nc.gpsimd.dma_start(
+            nc.scalar.dma_start(
                 wbs_raw[32 * q : 32 * q + 4, :, :],
                 wb_scales[:, 4 * q : 4 * q + 4, :].rearrange("a r c -> r a c").bitcast(I32),
             )
-        for a in range(PASSES):
-            nc.sync.dma_start(wa_raw[a][:], wa[512 * a : 512 * (a + 1), :].rearrange("(p i) c -> p i c", i=4))
+        nc.sync.dma_start(tabw[1][:], tab_words[1].rearrange("p t i -> p (t i)").bitcast(I32))
+        nc.vector.tensor_copy(v2g[:], tabs[:].bitcast(U8).indirect(list2[:]))
+        carry(v2g, v2s, nc.scalar)
+        wd_view = wd_words.rearrange("a p c i -> p a (c i)").bitcast(I32)
+        nc.sync.dma_start(wd_q[0][:], wd_view[:, :, 0:FIRST])
+        load_wa(0)
+        load_wa(1)
+        nc.vector.tensor_copy(v1g[:], tabs[:].bitcast(U8).indirect(list1[:]))
+        carry(v1g, v1s, nc.sync)
         wc_view = wc.rearrange("(g t e) n -> t g e n", t=4, e=8)
         for t in range(4):
             nc.sync.dma_start(wc_raw[0][:, t, :], wc_view[t][:, :, 0:FIRST])
@@ -115,34 +133,38 @@ def tile_list_connection_hold_scores_kernel(
         for t in range(4):
             nc.sync.dma_start(wc_raw[1][:, t, :], wc_view[t][:, :, FIRST:N])
 
-        def cols16(b):
-            return slice(b * HALF // 16, (b + 1) * HALF // 16)
-
-        def cols(b):
-            return slice(b * HALF, (b + 1) * HALF)
-
-        for picked, plane, lst, queue in ((v1g, v1s, list1, nc.scalar), (v2g, v2s, list2, nc.gpsimd)):
-            nc.vector.tensor_copy(picked[:], tabs[:].bitcast(U8).indirect(lst[:]))
-            for q in range(4):
-                queue.dma_start(
-                    plane[32 * q : 32 * q + 4, :].bitcast(I32).rearrange("r (a w) -> r a w", a=PASSES),
-                    picked[8 * q : 8 * q + 8, :].bitcast(I32),
-                )
-        nc.vector.tensor_copy(v1w[0][:], tabw[0][:].bitcast(U32).indirect(list1[:]))
         nc.vector.tensor_copy(v2w[0][:], tabw[0][:].bitcast(U32).indirect(list2[:]))
+        nc.scalar.copy(
+            wb_q[:].bitcast(U32).rearrange("p (a t g w) -> p a t g w", a=PASSES, t=4, w=4),
+            wb_raw[:].bitcast(U32).rearrange("p a (g t w) -> p a t g w", t=4, w=4),
+        )
+        nc.scalar.copy(
+            wb_s[:].bitcast(U32).rearrange("p (a t g w) -> p a t g w", a=PASSES, t=4, w=2),
+            wbs_raw[:].bitcast(U32).rearrange("p a (g t w) -> p a t g w", t=4, w=2),
+        )
+        nc.vector.tensor_copy(v1w[0][:], tabw[0][:].bitcast(U32).indirect(list1[:]))
+        for b in range(2):
+            nc.vector.tensor_copy(v2w[1][:, cols(b)], tabw[1][:].bitcast(U32).indirect(list2[:, cols16(b)]))
         for b in range(2):
             nc.vector.tensor_copy(v1w[1][:, cols(b)], tabw[1][:].bitcast(U32).indirect(list1[:, cols16(b)]))
 
-        nc.vector.tensor_copy(
-            wb_q[:].bitcast(I32).rearrange("p (a t g w) -> p a t g w", a=PASSES, t=4, w=4),
-            wb_raw[:].rearrange("p a (g t w) -> p a t g w", t=4, w=4),
-        )
-        nc.vector.tensor_copy(
-            wb_s[:].bitcast(I32).rearrange("p (a t g w) -> p a t g w", a=PASSES, t=4, w=2),
-            wbs_raw[:].rearrange("p a (g t w) -> p a t g w", t=4, w=2),
-        )
-        for b in range(2):
-            nc.vector.tensor_copy(v2w[1][:, cols(b)], tabw[1][:].bitcast(U32).indirect(list2[:, cols16(b)]))
+        for a in range(PASSES):
+            for c in range(S // CHUNK):
+                for t in range(4):
+                    c0 = a * H + t * P
+                    nc.tensor.matmul_mx(
+                        out=banks[c][:, t * CHUNK : (t + 1) * CHUNK],
+                        lhsT=wb_q[:, 2 * c0 : 2 * (c0 + P)].bitcast(FP4X4),
+                        lhsT_scale=wb_s[:, c0 : c0 + P],
+                        rhs=v2w[a][:, c * CHUNK : (c + 1) * CHUNK].bitcast(FP8X4),
+                        rhs_scale=v2s[:, a * S + c * CHUNK : a * S + (c + 1) * CHUNK],
+                        start=(a == 0 and t == 0),
+                        stop=(a == PASSES - 1 and t == 3),
+                    )
+        for c in range(S // CHUNK):
+            nc.scalar.copy(
+                dep_sb[c][:].rearrange("p (j t) -> p j t", t=4), banks[c][:].rearrange("p (t j) -> p j t", t=4)
+            )
 
         def part(i):
             u = 0 if i < GROUP else 1
@@ -153,7 +175,7 @@ def tile_list_connection_hold_scores_kernel(
                 for r in range(GROUP):
                     i = g * GROUP + r
                     u, ncols = part(i)
-                    bank = row_ps[2 * r + b]
+                    bank = banks[GROUP * b + r]
                     for a in range(PASSES):
                         nc.tensor.matmul_mx(
                             out=bank[:],
@@ -164,10 +186,9 @@ def tile_list_connection_hold_scores_kernel(
                             start=(a == 0),
                             stop=(a == PASSES - 1),
                         )
-                    nc.scalar.activation(damp[i % len(damp)][:, cols(b)], bank[:], ACT.Abs)
+                    nc.scalar.activation(logs[r][:, cols(b)], bank[:], ACT.Abs)
             for r in range(GROUP):
-                d = damp[(g * GROUP + r) % len(damp)]
-                nc.scalar.activation(d[:], d[:], ACT.Ln, bias=1.0)
+                nc.scalar.activation(logs[r][:], logs[r][:], ACT.Ln, bias=1.0)
 
         def round_wc(u, engine_copy):
             engine_copy(
@@ -180,37 +201,16 @@ def tile_list_connection_hold_scores_kernel(
 
         load_logs(0)
 
-        for a in range(PASSES):
-            nc.vector.tensor_copy(
-                wa_bf[a][:].rearrange("p (t g e i) -> p t g e i", t=4, e=8, i=4),
-                wa_raw[a][:].rearrange("p i (g t e) -> p t g e i", t=4, e=8),
-            )
+        rounded = [wa_bf[a][:].rearrange("p (t g e i) -> p t g e i", t=4, e=8, i=4) for a in range(PASSES)]
+        given = [wa_raw[a][:].rearrange("p i (g t e) -> p t g e i", t=4, e=8) for a in range(PASSES)]
+        for t in range(4):
+            nc.gpsimd.tensor_scalar(rounded[0][:, t], given[0][:, t], 1.0, 0.0, ALU.mult, ALU.add)
+        nc.vector.tensor_copy(rounded[1], given[1])
         for a in range(PASSES):
             nc.vector.quantize_mx(out=wa_q[a][:].bitcast(FP8X4), scales=wa_s[a][:], in_=wa_bf[a][:])
 
-        dep_banks = dep_ps + [r[:].rearrange("p (t j) -> p t j", t=4) for r in row_ps] + dep_ps
-
-        def departure(c):
-            bank = dep_banks[c]
-            for t in range(4):
-                for a in range(PASSES):
-                    c0 = a * H + t * P
-                    nc.tensor.matmul_mx(
-                        out=bank[:, t, :],
-                        lhsT=wb_q[:, 2 * c0 : 2 * (c0 + P)].bitcast(FP4X4),
-                        lhsT_scale=wb_s[:, c0 : c0 + P],
-                        rhs=v2w[a][:, c * CHUNK : (c + 1) * CHUNK].bitcast(FP8X4),
-                        rhs_scale=v2s[:, a * S + c * CHUNK : a * S + (c + 1) * CHUNK],
-                        start=(a == 0),
-                        stop=(a == PASSES - 1),
-                    )
-            nc.scalar.copy(dep_sb[c][:].rearrange("p (j t) -> p j t", t=4), bank[:].rearrange("p t j -> p j t"))
-
-        AHEAD = 6
-        for c in range(AHEAD):
-            departure(c)
         for c in range(S // CHUNK):
-            bank = feed_ps[c % 2]
+            bank = banks[4 + c % 4][:].rearrange("p (t j) -> p t j", t=4)
             for t in range(4):
                 for a in range(PASSES):
                     nc.tensor.matmul_mx(
@@ -222,12 +222,10 @@ def tile_list_connection_hold_scores_kernel(
                         start=(a == 0),
                         stop=(a == PASSES - 1),
                     )
-            if c + AHEAD < S // CHUNK:
-                departure(c + AHEAD)
             b, w = divmod(c, HALF // CHUNK)
             nc.vector.tensor_tensor(
                 h_bf[b][:, 4 * CHUNK * w : 4 * CHUNK * (w + 1)].rearrange("p (j t) -> p j t", t=4),
-                bank[:].rearrange("p t j -> p j t"),
+                bank.rearrange("p t j -> p j t"),
                 dep_sb[c][:].rearrange("p (j t) -> p j t", t=4),
                 ALU.min,
             )
@@ -240,24 +238,26 @@ def tile_list_connection_hold_scores_kernel(
         nc.vector.quantize_mx(out=h_q[1][:].bitcast(FP8X4), scales=h_s[1][:], in_=h_bf[1][:])
 
 
-        for n0 in range(0, widths[1], FIRST):
+        for n0 in range(0, widths[1], P):
             nc.gpsimd.tensor_scalar(
-                wc_bf[1][:, 4 * n0 : 4 * (n0 + FIRST)].rearrange("p (n t) -> p n t", t=4),
-                wc_raw[1][:, :, n0 : n0 + FIRST].rearrange("p t n -> p n t"),
+                wc_bf[1][:, 4 * n0 : 4 * (n0 + P)].rearrange("p (n t) -> p n t", t=4),
+                wc_raw[1][:, :, n0 : n0 + P].rearrange("p t n -> p n t"),
                 1.0,
                 0.0,
                 ALU.mult,
                 ALU.add,
             )
 
+        def factor(i, b):
+            return dep_sb[-(2 * i + b) % len(dep_sb)]
+
         def scores(g):
             for r in range(GROUP):
                 i = g * GROUP + r
                 u, ncols = part(i)
-                d = damp[i % len(damp)]
                 for b in range(2):
-                    nc.scalar.activation(d[:, cols(b)], d[:, cols(b)], ACT.Exp, scale=-1.0)
-                    bank = row_ps[2 * r + b]
+                    nc.scalar.activation(factor(i, b)[:], logs[r][:, cols(b)], ACT.Exp, scale=-1.0)
+                    bank = banks[GROUP * b + r]
                     nc.tensor.matmul_mx(
                         out=bank[:],
                         lhsT=wc_q[u][:, ncols].bitcast(FP8X4),
@@ -274,15 +274,16 @@ def tile_list_connection_hold_scores_kernel(
         def place(g):
             for r in range(GROUP):
                 i = g * GROUP + r
-                y = ys[i % len(ys)]
                 page = pages[i % PAGES]
                 for b in range(2):
-                    engine = nc.vector if (i, b) == (0, 0) else nc.gpsimd
-                    engine.tensor_tensor(
-                        y[:, cols(b)], hold[i % len(hold)][:, cols(b)], damp[i % len(damp)][:, cols(b)], ALU.mult
-                    )
-                    engine.tensor_tensor(y[:, cols(b)], y[:, cols(b)], gain[:, cols(b)], ALU.mult)
-                    nc.vector.tensor_copy(page[:].indirect(list3[:, cols16(b)]), y[:, cols(b)])
+                    f, y, score = factor(i, b)[:], ys[:, cols(b)], hold[i % len(hold)][:, cols(b)]
+                    if (i, b) == (0, 0):
+                        nc.vector.tensor_tensor(y, f, gain[:, cols(b)], ALU.mult)
+                        nc.vector.tensor_tensor(y, y, score, ALU.mult)
+                    else:
+                        nc.gpsimd.tensor_tensor(f, f, gain[:, cols(b)], ALU.mult)
+                        nc.gpsimd.tensor_tensor(y, f, score, ALU.mult)
+                    nc.vector.tensor_copy(page[:].indirect(list3[:, cols16(b)]), ys[:, cols(b)])
                 nc.sync.dma_start(out[i * P : (i + 1) * P, :], page[:])
                 if i == 0:
                     quantise_wc(1)

@@ -59,26 +59,28 @@ def tile_list_connection_hold_scores_kernel(
         widths = [FIRST, N - FIRST]
         starts = [0, FIRST]
         wc_raw = [sb("wc_raw%d" % u, [P, 4, widths[u]], F32) for u in range(2)]
-        wc_q = [sb("wc_q0", [P, FIRST], U32), wa_q[0]]
-        wc_s = [sb("wc_s0", [P, FIRST], U8), wa_s[0]]
+        wc_q = [sb("wc_q%d" % g, [P, FIRST], U32) for g in range(ROW_TILES // GROUP)]
+        wc_s = [sb("wc_s%d" % g, [P, FIRST], U8) for g in range(ROW_TILES // GROUP)]
         wd_q = [sb("wd_q%d" % u, [P, PASSES, widths[u]], I32) for u in range(2)]
         wd_s = sb("wd_s", [P, PASSES * N], U8)
         bias = sb("bias", [P, ROW_TILES], F32)
         gain = sb("gain", [P, S], F32)
         dep_sb = [sb("dep_sb%d" % c, [P, 4 * CHUNK], F32) for c in range(S // CHUNK)]
         h_bf = [sb("h_bf%d" % b, [P, 4 * HALF], BF16) for b in range(2)]
-        wc_bf = [sb("wc_bf%d" % u, [P, 4 * widths[u]], BF16) for u in range(2)]
         h_q = [sb("h_q%d" % b, [P, HALF], U32) for b in range(2)]
         h_s = [sb("h_s%d" % b, [P, HALF], U8) for b in range(2)]
         logs = [sb("logs%d" % i, [P, S], F32) for i in range(GROUP)]
         hold = [sb("hold%d" % i, [P, S], F32) for i in range(2 * GROUP)]
-        ys = h_bf[1][:].bitcast(F32)
+        ys = [h_bf[1][:].bitcast(F32), h_bf[0][:].bitcast(F32)]
+        wc_bf = [sb("wc_bf0", [P, 4 * FIRST], BF16)[:], dep_sb[0][:].bitcast(BF16), dep_sb[-1][:].bitcast(BF16)]
         pages = [sb("page%d" % i, [P, T2], F32) for i in range(PAGES)]
         banks = [psum.tile([P, HALF], F32, name="bank%d" % i) for i in range(8)]
 
         nc.vector.memset(wbs_raw[:], 0)
         nc.vector.memset(tabs[32:64, :], 0)
         nc.vector.memset(tabs[64:P, :], 0)
+        for page in pages:
+            nc.vector.memset(page[:], 0.0)
 
         def cols16(b):
             return slice(b * HALF // 16, (b + 1) * HALF // 16)
@@ -86,9 +88,9 @@ def tile_list_connection_hold_scores_kernel(
         def cols(b):
             return slice(b * HALF, (b + 1) * HALF)
 
-        def carry(picked, plane, queue):
+        def carry(picked, plane):
             for q in range(4):
-                queue.dma_start(
+                nc.sync.dma_start(
                     plane[32 * q : 32 * q + 4, :].bitcast(I32).rearrange("r (a w) -> r a w", a=PASSES),
                     picked[8 * q : 8 * q + 8, :].bitcast(I32),
                 )
@@ -106,8 +108,6 @@ def tile_list_connection_hold_scores_kernel(
                 wd_s[32 * q : 32 * q + 4, :].rearrange("r (a c) -> r a c", a=PASSES).bitcast(I32),
                 wd_scales[:, 4 * q : 4 * q + 4, :].rearrange("a r c -> r a c").bitcast(I32),
             )
-        for page in pages:
-            nc.gpsimd.memset(page[:], 0.0)
         for q in range(4):
             nc.scalar.dma_start(
                 wbs_raw[32 * q : 32 * q + 4, :, :],
@@ -115,13 +115,13 @@ def tile_list_connection_hold_scores_kernel(
             )
         nc.sync.dma_start(tabw[1][:], tab_words[1].rearrange("p t i -> p (t i)").bitcast(I32))
         nc.vector.tensor_copy(v2g[:], tabs[:].bitcast(U8).indirect(list2[:]))
-        carry(v2g, v2s, nc.scalar)
+        carry(v2g, v2s)
         wd_view = wd_words.rearrange("a p c i -> p a (c i)").bitcast(I32)
         nc.sync.dma_start(wd_q[0][:], wd_view[:, :, 0:FIRST])
         load_wa(0)
         load_wa(1)
         nc.vector.tensor_copy(v1g[:], tabs[:].bitcast(U8).indirect(list1[:]))
-        carry(v1g, v1s, nc.sync)
+        carry(v1g, v1s)
         wc_view = wc.rearrange("(g t e) n -> t g e n", t=4, e=8)
         for t in range(4):
             nc.sync.dma_start(wc_raw[0][:, t, :], wc_view[t][:, :, 0:FIRST])
@@ -190,22 +190,24 @@ def tile_list_connection_hold_scores_kernel(
             for r in range(GROUP):
                 nc.scalar.activation(logs[r][:], logs[r][:], ACT.Ln, bias=1.0)
 
-        def round_wc(u, engine_copy):
+        def round_wc(g, engine_copy):
+            u = min(g, 1)
+            n0 = g * FIRST - starts[u]
             engine_copy(
-                wc_bf[u][:].rearrange("p (n t) -> p n t", t=4),
-                wc_raw[u][:].rearrange("p t n -> p n t"),
+                wc_bf[g].rearrange("p (n t) -> p n t", t=4),
+                wc_raw[u][:, :, n0 : n0 + FIRST].rearrange("p t n -> p n t"),
             )
 
-        def quantise_wc(u):
-            nc.vector.quantize_mx(out=wc_q[u][:].bitcast(FP8X4), scales=wc_s[u][:], in_=wc_bf[u][:])
+        def quantise_wc(g):
+            nc.vector.quantize_mx(out=wc_q[g][:].bitcast(FP8X4), scales=wc_s[g][:], in_=wc_bf[g])
 
         load_logs(0)
 
-        rounded = [wa_bf[a][:].rearrange("p (t g e i) -> p t g e i", t=4, e=8, i=4) for a in range(PASSES)]
-        given = [wa_raw[a][:].rearrange("p i (g t e) -> p t g e i", t=4, e=8) for a in range(PASSES)]
-        for t in range(4):
-            nc.gpsimd.tensor_scalar(rounded[0][:, t], given[0][:, t], 1.0, 0.0, ALU.mult, ALU.add)
-        nc.vector.tensor_copy(rounded[1], given[1])
+        for a in range(PASSES):
+            nc.vector.tensor_copy(
+                wa_bf[a][:].rearrange("p (t g e i) -> p t g e i", t=4, e=8, i=4),
+                wa_raw[a][:].rearrange("p i (g t e) -> p t g e i", t=4, e=8),
+            )
         for a in range(PASSES):
             nc.vector.quantize_mx(out=wa_q[a][:].bitcast(FP8X4), scales=wa_s[a][:], in_=wa_bf[a][:])
 
@@ -238,30 +240,19 @@ def tile_list_connection_hold_scores_kernel(
         nc.vector.quantize_mx(out=h_q[1][:].bitcast(FP8X4), scales=h_s[1][:], in_=h_bf[1][:])
 
 
-        for n0 in range(0, widths[1], P):
-            nc.gpsimd.tensor_scalar(
-                wc_bf[1][:, 4 * n0 : 4 * (n0 + P)].rearrange("p (n t) -> p n t", t=4),
-                wc_raw[1][:, :, n0 : n0 + P].rearrange("p t n -> p n t"),
-                1.0,
-                0.0,
-                ALU.mult,
-                ALU.add,
-            )
-
         def factor(i, b):
             return dep_sb[-(2 * i + b) % len(dep_sb)]
 
         def scores(g):
             for r in range(GROUP):
                 i = g * GROUP + r
-                u, ncols = part(i)
                 for b in range(2):
                     nc.scalar.activation(factor(i, b)[:], logs[r][:, cols(b)], ACT.Exp, scale=-1.0)
-                    bank = banks[GROUP * b + r]
+                    bank = banks[r + b]
                     nc.tensor.matmul_mx(
                         out=bank[:],
-                        lhsT=wc_q[u][:, ncols].bitcast(FP8X4),
-                        lhsT_scale=wc_s[u][:, ncols],
+                        lhsT=wc_q[g][:, r * P : (r + 1) * P].bitcast(FP8X4),
+                        lhsT_scale=wc_s[g][:, r * P : (r + 1) * P],
                         rhs=h_q[b][:].bitcast(FP8X4),
                         rhs_scale=h_s[b][:],
                         start=True,
@@ -271,25 +262,22 @@ def tile_list_connection_hold_scores_kernel(
                         hold[i % len(hold)][:, cols(b)], bank[:], ACT.Tanh, bias=bias[:, i : i + 1]
                     )
 
-        def place(g):
-            for r in range(GROUP):
-                i = g * GROUP + r
-                page = pages[i % PAGES]
-                for b in range(2):
-                    f, y, score = factor(i, b)[:], ys[:, cols(b)], hold[i % len(hold)][:, cols(b)]
-                    if (i, b) == (0, 0):
-                        nc.vector.tensor_tensor(y, f, gain[:, cols(b)], ALU.mult)
-                        nc.vector.tensor_tensor(y, y, score, ALU.mult)
-                    else:
-                        nc.gpsimd.tensor_tensor(f, f, gain[:, cols(b)], ALU.mult)
-                        nc.gpsimd.tensor_tensor(y, f, score, ALU.mult)
-                    nc.vector.tensor_copy(page[:].indirect(list3[:, cols16(b)]), ys[:, cols(b)])
-                nc.sync.dma_start(out[i * P : (i + 1) * P, :], page[:])
-                if i == 0:
-                    quantise_wc(1)
+        def place(i):
+            page, y = pages[i % PAGES], ys[i % 2]
+            for b in range(2):
+                nc.vector.tensor_tensor(y[:, cols(b)], hold[i % len(hold)][:, cols(b)], factor(i, b)[:], ALU.mult)
+                nc.vector.tensor_tensor(
+                    page[:].indirect(list3[:, cols16(b)]), y[:, cols(b)], gain[:, cols(b)], ALU.mult
+                )
+            nc.sync.dma_start(out[i * P : (i + 1) * P, :], page[:])
 
-        for g in range(ROW_TILES // GROUP):
+        scores(0)
+        place(0)
+        for g in range(1, ROW_TILES // GROUP):
+            round_wc(g, nc.scalar.copy)
+            quantise_wc(g)
+            load_logs(g)
+            place(g * GROUP - 1)
             scores(g)
-            if g + 1 < ROW_TILES // GROUP:
-                load_logs(g + 1)
-            place(g)
+            place(g * GROUP)
+        place(ROW_TILES - 1)

@@ -77,10 +77,10 @@ def tile_list_connection_hold_scores_kernel(
         banks = [psum.tile([P, HALF], F32, name="bank%d" % i) for i in range(8)]
 
         nc.vector.memset(wbs_raw[:], 0)
-        nc.vector.memset(tabs[32:64, :], 0)
-        nc.vector.memset(tabs[64:P, :], 0)
-        for page in pages:
-            nc.vector.memset(page[:], 0.0)
+        nc.gpsimd.memset(tabs[32:64, :], 0)
+        nc.gpsimd.memset(tabs[64:P, :], 0)
+        nc.vector.memset(pages[0][:], 0.0)
+        nc.gpsimd.memset(pages[1][:], 0.0)
 
         def cols16(b):
             return slice(b * HALF // 16, (b + 1) * HALF // 16)
@@ -148,9 +148,9 @@ def tile_list_connection_hold_scores_kernel(
         for b in range(2):
             nc.vector.tensor_copy(v1w[1][:, cols(b)], tabw[1][:].bitcast(U32).indirect(list1[:, cols16(b)]))
 
-        for a in range(PASSES):
-            for c in range(S // CHUNK):
-                for t in range(4):
+        for c in range(S // CHUNK):
+            for t in range(4):
+                for a in range(PASSES):
                     c0 = a * H + t * P
                     nc.tensor.matmul_mx(
                         out=banks[c][:, t * CHUNK : (t + 1) * CHUNK],
@@ -158,10 +158,9 @@ def tile_list_connection_hold_scores_kernel(
                         lhsT_scale=wb_s[:, c0 : c0 + P],
                         rhs=v2w[a][:, c * CHUNK : (c + 1) * CHUNK].bitcast(FP8X4),
                         rhs_scale=v2s[:, a * S + c * CHUNK : a * S + (c + 1) * CHUNK],
-                        start=(a == 0 and t == 0),
-                        stop=(a == PASSES - 1 and t == 3),
+                        start=(a == 0),
+                        stop=(a == PASSES - 1),
                     )
-        for c in range(S // CHUNK):
             nc.scalar.copy(
                 dep_sb[c][:].rearrange("p (j t) -> p j t", t=4), banks[c][:].rearrange("p (t j) -> p j t", t=4)
             )
@@ -266,9 +265,12 @@ def tile_list_connection_hold_scores_kernel(
             page, y = pages[i % PAGES], ys[i % 2]
             for b in range(2):
                 nc.vector.tensor_tensor(y[:, cols(b)], hold[i % len(hold)][:, cols(b)], factor(i, b)[:], ALU.mult)
-                nc.vector.tensor_tensor(
-                    page[:].indirect(list3[:, cols16(b)]), y[:, cols(b)], gain[:, cols(b)], ALU.mult
-                )
+                if i == 0:
+                    nc.vector.tensor_tensor(
+                        page[:].indirect(list3[:, cols16(b)]), y[:, cols(b)], gain[:, cols(b)], ALU.mult
+                    )
+            if i > 0:
+                nc.vector.tensor_tensor(page[:].indirect(list3[:]), y, gain[:], ALU.mult)
             nc.sync.dma_start(out[i * P : (i + 1) * P, :], page[:])
 
         scores(0)

from contextlib import ExitStack

import concourse.mybir as mybir

K, T, H, N, S, T2 = 1024, 4096, 512, 768, 1024, 2048
FLOPS = 2 * S * (K * H + K * H + K * N + H * N)

F32 = mybir.dt.float32
BF16 = mybir.dt.bfloat16
I32 = mybir.dt.int32
U32 = mybir.dt.uint32
U16 = mybir.dt.uint16
U8 = mybir.dt.uint8
FP8X4 = mybir.dt.float8_e4m3fn_x4
FP4X4 = mybir.dt.float4_e2m1fn_x4
ACT = mybir.ActivationFunctionType
ALU = mybir.AluOpType

P = 128
PASSES = K // 512
HALF = 512
CHUNK = 128
ROW_TILES = N // P
GROUP = 2
FIRST = GROUP * P
PAGES = 2


def tile_list_connection_hold_scores_kernel(
    tc, tab_words, tab_scales, wa, wb_words, wb_scales, wc, bc, wd_words, wd_scales, wgo, offs, offs2, offs3, out
):
    nc = tc.nc
    with ExitStack() as ctx:
        keep = ctx.enter_context(tc.tile_pool(name="keep", bufs=1))
        psum = ctx.enter_context(tc.psum_pool(name="psum", bufs=1))

        def sb(name, shape, dtype):
            return keep.tile(shape, dtype, name=name, align_bytes=64)

        list1 = keep.tile([P, S // 16], U16, name="list1")
        list2 = keep.tile([P, S // 16], U16, name="list2")
        list3 = keep.tile([P, S // 16], U16, name="list3")
        tabw = [sb("tabw%d" % a, [P, T], I32) for a in range(PASSES)]
        tabs = sb("tabs", [P, T // 4], I32)
        v1w = [sb("v1w%d" % a, [P, S], U32) for a in range(PASSES)]
        v2w = [sb("v2w%d" % a, [P, S], U32) for a in range(PASSES)]
        v1g = sb("v1g", [P, S], U8)
        v2g = sb("v2g", [P, S], U8)
        v1s = sb("v1s", [P, PASSES * S], U8)
        v2s = sb("v2s", [P, PASSES * S], U8)
        wa_raw = [sb("wa_raw%d" % a, [P, 4, H], F32) for a in range(PASSES)]
        wa_bf = [sb("wa_bf%d" % a, [P, 4 * H], BF16) for a in range(PASSES)]
        wa_q = [sb("wa_q%d" % a, [P, H], U32) for a in range(PASSES)]
        wa_s = [sb("wa_s%d" % a, [P, H], U8) for a in range(PASSES)]
        wb_raw = sb("wb_raw", [P, PASSES, H // 2], I32)
        wbs_raw = sb("wbs_raw", [P, PASSES, H // 4], I32)
        wb_q = sb("wb_q", [P, PASSES * 2 * H], U8)
        wb_s = sb("wb_s", [P, PASSES * H], U8)
        widths = [FIRST, N - FIRST]
        starts = [0, FIRST]
        wc_raw = [sb("wc_raw%d" % u, [P, 4, widths[u]], F32) for u in range(2)]
        wc_q = [sb("wc_q%d" % g, [P, FIRST], U32) for g in range(ROW_TILES // GROUP)]
        wc_s = [sb("wc_s%d" % g, [P, FIRST], U8) for g in range(ROW_TILES // GROUP)]
        wd_q = [sb("wd_q%d" % u, [P, PASSES, widths[u]], I32) for u in range(2)]
        wd_s = sb("wd_s", [P, PASSES * N], U8)
        bias = sb("bias", [P, ROW_TILES], F32)
        gain = sb("gain", [P, S], F32)
        dep_sb = [sb("dep_sb%d" % c, [P, 4 * CHUNK], F32) for c in range(S // CHUNK)]
        h_bf = [sb("h_bf%d" % b, [P, 4 * HALF], BF16) for b in range(2)]
        h_q = [sb("h_q%d" % b, [P, HALF], U32) for b in range(2)]
        h_s = [sb("h_s%d" % b, [P, HALF], U8) for b in range(2)]
        logs = [sb("logs%d" % i, [P, S], F32) for i in range(GROUP)]
        hold = [sb("hold%d" % i, [P, S], F32) for i in range(2 * GROUP)]
        ys = [h_bf[1][:].bitcast(F32), h_bf[0][:].bitcast(F32)]
        wc_bf = [sb("wc_bf0", [P, 4 * FIRST], BF16)[:], dep_sb[0][:].bitcast(BF16), dep_sb[-1][:].bitcast(BF16)]
        pages = [sb("page%d" % i, [P, T2], F32) for i in range(PAGES)]
        banks = [psum.tile([P, HALF], F32, name="bank%d" % i) for i in range(8)]

        nc.vector.memset(wbs_raw[:], 0)
        nc.gpsimd.memset(tabs[32:64, :], 0)
        nc.gpsimd.memset(tabs[64:P, :], 0)
        nc.vector.memset(pages[0][:], 0.0)
        nc.gpsimd.memset(pages[1][:], 0.0)

        def cols16(b):
            return slice(b * HALF // 16, (b + 1) * HALF // 16)

        def cols(b):
            return slice(b * HALF, (b + 1) * HALF)

        def carry(picked, plane):
            for q in range(4):
                nc.sync.dma_start(
                    plane[32 * q : 32 * q + 4, :].bitcast(I32).rearrange("r (a w) -> r a w", a=PASSES),
                    picked[8 * q : 8 * q + 8, :].bitcast(I32),
                )

        def load_wa(a):
            nc.sync.dma_start(wa_raw[a][:], wa[512 * a : 512 * (a + 1), :].rearrange("(p i) c -> p i c", i=4))

        nc.sync.dma_start(tabs[0:32, :], tab_scales.rearrange("a q c -> q a c").bitcast(I32))
        nc.sync.dma_start(list2[:], offs2)
        nc.sync.dma_start(list1[:], offs)
        nc.sync.dma_start(wb_raw[:], wb_words.rearrange("a p c -> p a c").bitcast(I32))
        nc.sync.dma_start(tabw[0][:], tab_words[0].rearrange("p t i -> p (t i)").bitcast(I32))
        for q in range(4):
            nc.gpsimd.dma_start(
                wd_s[32 * q : 32 * q + 4, :].rearrange("r (a c) -> r a c", a=PASSES).bitcast(I32),
                wd_scales[:, 4 * q : 4 * q + 4, :].rearrange("a r c -> r a c").bitcast(I32),
            )
        for q in range(4):
            nc.scalar.dma_start(
                wbs_raw[32 * q : 32 * q + 4, :, :],
                wb_scales[:, 4 * q : 4 * q + 4, :].rearrange("a r c -> r a c").bitcast(I32),
            )
        nc.sync.dma_start(tabw[1][:], tab_words[1].rearrange("p t i -> p (t i)").bitcast(I32))
        nc.vector.tensor_copy(v2g[:], tabs[:].bitcast(U8).indirect(list2[:]))
        carry(v2g, v2s)
        wd_view = wd_words.rearrange("a p c i -> p a (c i)").bitcast(I32)
        nc.sync.dma_start(wd_q[0][:], wd_view[:, :, 0:FIRST])
        load_wa(0)
        load_wa(1)
        nc.vector.tensor_copy(v1g[:], tabs[:].bitcast(U8).indirect(list1[:]))
        carry(v1g, v1s)
        wc_view = wc.rearrange("(g t e) n -> t g e n", t=4, e=8)
        for t in range(4):
            nc.sync.dma_start(wc_raw[0][:, t, :], wc_view[t][:, :, 0:FIRST])
        nc.sync.dma_start(gain[:], wgo)
        nc.sync.dma_start(list3[:], offs3)
        with nc.allow_non_contiguous_dma(reason="one bias value a partition and row tile"):
            nc.sync.dma_start(bias[:], bc.rearrange("(i p) -> p i", p=P))
        nc.sync.dma_start(wd_q[1][:], wd_view[:, :, FIRST:N])
        for t in range(4):
            nc.sync.dma_start(wc_raw[1][:, t, :], wc_view[t][:, :, FIRST:N])

        nc.vector.tensor_copy(v2w[0][:], tabw[0][:].bitcast(U32).indirect(list2[:]))
        nc.scalar.copy(
            wb_q[:].bitcast(U32).rearrange("p (a t g w) -> p a t g w", a=PASSES, t=4, w=4),
            wb_raw[:].bitcast(U32).rearrange("p a (g t w) -> p a t g w", t=4, w=4),
        )
        nc.scalar.copy(
            wb_s[:].bitcast(U32).rearrange("p (a t g w) -> p a t g w", a=PASSES, t=4, w=2),
            wbs_raw[:].bitcast(U32).rearrange("p a (g t w) -> p a t g w", t=4, w=2),
        )
        nc.vector.tensor_copy(v1w[0][:], tabw[0][:].bitcast(U32).indirect(list1[:]))
        for b in range(2):
            nc.vector.tensor_copy(v2w[1][:, cols(b)], tabw[1][:].bitcast(U32).indirect(list2[:, cols16(b)]))
        for b in range(2):
            nc.vector.tensor_copy(v1w[1][:, cols(b)], tabw[1][:].bitcast(U32).indirect(list1[:, cols16(b)]))

        for c in range(S // CHUNK):
            for t in range(4):
                for a in range(PASSES):
                    c0 = a * H + t * P
                    nc.tensor.matmul_mx(
                        out=banks[c][:, t * CHUNK : (t + 1) * CHUNK],
                        lhsT=wb_q[:, 2 * c0 : 2 * (c0 + P)].bitcast(FP4X4),
                        lhsT_scale=wb_s[:, c0 : c0 + P],
                        rhs=v2w[a][:, c * CHUNK : (c + 1) * CHUNK].bitcast(FP8X4),
                        rhs_scale=v2s[:, a * S + c * CHUNK : a * S + (c + 1) * CHUNK],
                        start=(a == 0),
                        stop=(a == PASSES - 1),
                    )
            nc.scalar.copy(
                dep_sb[c][:].rearrange("p (j t) -> p j t", t=4), banks[c][:].rearrange("p (t j) -> p j t", t=4)
            )

        def part(i):
            u = 0 if i < GROUP else 1
            return u, slice(i * P - starts[u], (i + 1) * P - starts[u])

        def load_logs(g):
            for b in range(2):
                for r in range(GROUP):
                    i = g * GROUP + r
                    u, ncols = part(i)
                    bank = banks[GROUP * b + r]
                    for a in range(PASSES):
                        nc.tensor.matmul_mx(
                            out=bank[:],
                            lhsT=wd_q[u][:, a, ncols].bitcast(FP8X4),
                            lhsT_scale=wd_s[:, a * N + i * P : a * N + (i + 1) * P],
                            rhs=v1w[a][:, cols(b)].bitcast(FP8X4),
                            rhs_scale=v1s[:, a * S + b * HALF : a * S + (b + 1) * HALF],
                            start=(a == 0),
                            stop=(a == PASSES - 1),
                        )
                    nc.scalar.activation(logs[r][:, cols(b)], bank[:], ACT.Abs)
            for r in range(GROUP):
                nc.scalar.activation(logs[r][:], logs[r][:], ACT.Ln, bias=1.0)

        def round_wc(g, engine_copy):
            u = min(g, 1)
            n0 = g * FIRST - starts[u]
            engine_copy(
                wc_bf[g].rearrange("p (n t) -> p n t", t=4),
                wc_raw[u][:, :, n0 : n0 + FIRST].rearrange("p t n -> p n t"),
            )

        def quantise_wc(g):
            nc.vector.quantize_mx(out=wc_q[g][:].bitcast(FP8X4), scales=wc_s[g][:], in_=wc_bf[g])

        load_logs(0)

        for a in range(PASSES):
            nc.vector.tensor_copy(
                wa_bf[a][:].rearrange("p (t g e i) -> p t g e i", t=4, e=8, i=4),
                wa_raw[a][:].rearrange("p i (g t e) -> p t g e i", t=4, e=8),
            )
        for a in range(PASSES):
            nc.vector.quantize_mx(out=wa_q[a][:].bitcast(FP8X4), scales=wa_s[a][:], in_=wa_bf[a][:])

        for c in range(S // CHUNK):
            bank = banks[4 + c % 4][:].rearrange("p (t j) -> p t j", t=4)
            for t in range(4):
                for a in range(PASSES):
                    nc.tensor.matmul_mx(
                        out=bank[:, t, :],
                        lhsT=wa_q[a][:, t * P : (t + 1) * P].bitcast(FP8X4),
                        lhsT_scale=wa_s[a][:, t * P : (t + 1) * P],
                        rhs=v1w[a][:, c * CHUNK : (c + 1) * CHUNK].bitcast(FP8X4),
                        rhs_scale=v1s[:, a * S + c * CHUNK : a * S + (c + 1) * CHUNK],
                        start=(a == 0),
                        stop=(a == PASSES - 1),
                    )
            b, w = divmod(c, HALF // CHUNK)
            nc.vector.tensor_tensor(
                h_bf[b][:, 4 * CHUNK * w : 4 * CHUNK * (w + 1)].rearrange("p (j t) -> p j t", t=4),
                bank.rearrange("p t j -> p j t"),
                dep_sb[c][:].rearrange("p (j t) -> p j t", t=4),
                ALU.min,
            )
            if c == 0:
                round_wc(0, nc.vector.tensor_copy)
            if c == 1:
                quantise_wc(0)
            if c == HALF // CHUNK:
                nc.vector.quantize_mx(out=h_q[0][:].bitcast(FP8X4), scales=h_s[0][:], in_=h_bf[0][:])
        nc.vector.quantize_mx(out=h_q[1][:].bitcast(FP8X4), scales=h_s[1][:], in_=h_bf[1][:])


        def factor(i, b):
            return dep_sb[-(2 * i + b) % len(dep_sb)]

        def scores(g):
            for r in range(GROUP):
                i = g * GROUP + r
                for b in range(2):
                    nc.scalar.activation(factor(i, b)[:], logs[r][:, cols(b)], ACT.Exp, scale=-1.0)
                    bank = banks[r + b]
                    nc.tensor.matmul_mx(
                        out=bank[:],
                        lhsT=wc_q[g][:, r * P : (r + 1) * P].bitcast(FP8X4),
                        lhsT_scale=wc_s[g][:, r * P : (r + 1) * P],
                        rhs=h_q[b][:].bitcast(FP8X4),
                        rhs_scale=h_s[b][:],
                        start=True,
                        stop=True,
                    )
                    nc.scalar.activation(
                        hold[i % len(hold)][:, cols(b)], bank[:], ACT.Tanh, bias=bias[:, i : i + 1]
                    )

        def place(i):
            page, y = pages[i % PAGES], ys[i % 2]
            for b in range(2):
                nc.vector.tensor_tensor(y[:, cols(b)], hold[i % len(hold)][:, cols(b)], factor(i, b)[:], ALU.mult)
                if i == 0:
                    nc.vector.tensor_tensor(
                        page[:].indirect(list3[:, cols16(b)]), y[:, cols(b)], gain[:, cols(b)], ALU.mult
                    )
            if i > 0:
                nc.vector.tensor_tensor(page[:].indirect(list3[:]), y, gain[:], ALU.mult)
            nc.sync.dma_start(out[i * P : (i + 1) * P, :], page[:])

        scores(0)
        place(0)
        for g in range(1, ROW_TILES // GROUP):
            round_wc(g, nc.scalar.copy)
            quantise_wc(g)
            load_logs(g)
            place(g * GROUP - 1)
            scores(g)
            place(g * GROUP)
        place(ROW_TILES - 1)
